import numpy as np
import ml_dtypes


def mxq(x, axis, fmt="e4m3"):
    dtype, down = {"e4m3": (ml_dtypes.float8_e4m3fn, 7), "e5m2": (ml_dtypes.float8_e5m2, 14)}[fmt]
    v = np.moveaxis(np.asarray(x, np.float32).astype(ml_dtypes.bfloat16).astype(np.float64), axis, -1)
    blocks = v.reshape(v.shape[:-1] + (-1, 32))
    amax = np.abs(blocks).max(-1, keepdims=True)
    byte = np.maximum(np.where(amax > 0, np.frexp(amax)[1] - 1 + 127, 0) - down, 1)
    scale = np.exp2(byte - 127.0)
    codes = (blocks / scale).astype(np.float32).astype(dtype).astype(np.float64)
    return np.moveaxis((codes * scale).reshape(v.shape), -1, axis)


WIDE = False


def mx_kscale(k):
    if not WIDE:
        return np.ones(k)
    levels = np.array([10, -10, 5, -5, 0])
    if k % 512:
        return np.exp2(np.random.permutation(np.resize(levels, k // 32))).repeat(32)
    a = np.empty((k // 512, 16))
    for p in range(k // 512):
        a[p, :8] = np.random.permutation(np.resize(levels, 8))
        for g in range(8):
            far = levels[np.abs(levels - a[p, g]) >= 10]
            a[p, g + 8] = far[np.random.randint(len(far))]
    return np.exp2(a.ravel()).repeat(32)


def f64(x):
    return np.asarray(x).astype(np.float64)


def striped8(idx):
    return np.asarray(idx).reshape(8, -1, 16).transpose(0, 2, 1).reshape(128, -1).astype(np.uint16)


def unstriped8(offs):
    return offs.reshape(8, 16, -1).transpose(0, 2, 1).reshape(8, -1).astype(np.int64)


def pick8(x, idx, run):
    r = np.arange(len(x))
    return x[r[:, None], idx[r % (8 * run) // run]]


E2M1 = np.array([0.0, 0.5, 1.0, 1.5, 2.0, 3.0, 4.0, 6.0, -0.0, -0.5, -1.0, -1.5, -2.0, -3.0, -4.0, -6.0])


def pack_weight(w, fmt):
    k, n = w.shape
    w = f64(np.asarray(w, np.float32).astype(ml_dtypes.bfloat16)).reshape(k // 32, 32, n)
    amax = np.abs(w).max(1)
    if fmt == "e4m3":
        byte = np.frexp(amax)[1] - 1 + 127 - 7
    else:
        mant, ex = np.frexp(amax / 6.0)
        byte = np.where(mant > 0.5, ex, ex - 1) + 127
    byte = np.clip(np.where(amax > 0, byte, 1), 1, 254)
    scaled = (w * np.exp2(127.0 - byte)[:, None, :]).reshape(k, n).astype(np.float32)
    by_word = np.ascontiguousarray(scaled.reshape(k // 512, 128, 4, n).transpose(0, 1, 3, 2))
    if fmt == "e4m3":
        words = by_word.astype(ml_dtypes.float8_e4m3fn).view(np.uint8)
    else:
        c = by_word.astype(ml_dtypes.float4_e2m1fn).view(np.uint8) & 0xF
        words = (c[..., 0::2] | (c[..., 1::2] << 4)).reshape(k // 512, 128, 2 * n)
    return np.ascontiguousarray(words), np.ascontiguousarray(byte.astype(np.uint8).reshape(k // 512, 16, n))


def unpack_weight(words, scales, fmt):
    g, _, n = scales.shape
    words = np.ascontiguousarray(words).reshape(g, 128, n, -1)
    if fmt == "e4m3":
        vals = words.view(ml_dtypes.float8_e4m3fn).astype(np.float64)
    else:
        nib = np.empty((g, 128, n, 4), np.uint8)
        nib[..., 0::2] = words & 0xF
        nib[..., 1::2] = words >> 4
        vals = E2M1[nib]
    vals = vals * np.repeat(np.exp2(scales.astype(np.float64) - 127.0), 8, axis=1)[..., None]
    return vals.transpose(0, 1, 3, 2).reshape(g * 512, n)


D, K, T, U, I, Q = 512, 512, 1024, 1024, 512, 128


def setup_inputs():
    n = np.random.standard_normal
    idx = np.stack([np.random.permutation(T)[:I] for _ in range(8)])
    idx2 = np.stack([np.random.permutation(U)[:I] for _ in range(8)])
    idx3 = np.stack([np.random.permutation(T)[:I] for _ in range(8)])
    idx4 = np.stack([np.random.permutation(U)[:I] for _ in range(8)])
    idx5 = np.stack([np.random.permutation(U)[:I] for _ in range(8)])
    fd = mx_kscale(D)
    fk = mx_kscale(K)
    wqp = pack_weight(n((D, K)) * 1.0 / np.sqrt(D) * fd[:, None] * fk, "e4m3")
    keysp = pack_weight(n((K, T)) * 1.0 / np.sqrt(K) / fk[:, None], "e4m3")
    notesp = pack_weight(n((K, U)) * 1.0 / np.sqrt(K) / fk[:, None], "e2m1")
    return {
        "states": (n((D, Q)) * 0.95 / fd[:, None]).astype(np.float32),
        "wq_words": wqp[0],
        "wq_scales": wqp[1],
        "keys_words": keysp[0],
        "keys_scales": keysp[1],
        "notes_words": notesp[0],
        "notes_scales": notesp[1],
        "offs": striped8(idx),
        "offs2": striped8(idx2),
        "offs3": striped8(idx3),
        "offs4": striped8(idx4),
        "offs5": striped8(idx5),
    }


def reference(states, wq_words, wq_scales, keys_words, keys_scales, notes_words, notes_scales, offs, offs2, offs3, offs4, offs5):
    idx = unstriped8(offs)
    idx2 = unstriped8(offs2)
    idx3 = unstriped8(offs3)
    idx4 = unstriped8(offs4)
    idx5 = unstriped8(offs5)
    wqu = unpack_weight(wq_words, wq_scales, "e4m3")
    keysu = unpack_weight(keys_words, keys_scales, "e4m3")
    notesu = unpack_weight(notes_words, notes_scales, "e2m1")
    statesq = mxq(f64(states), 0, "e4m3")
    qv = wqu.T @ statesq
    qvq = mxq(qv, 0, "e4m3")
    a = qvq.T @ keysu
    b = qvq.T @ notesu
    f1 = np.zeros((Q, U))
    f1[np.arange(Q)[:, None], idx2[np.arange(Q) % 128 // 16]] = pick8(a, idx, 16)
    f2 = np.zeros((Q, U))
    f2[np.arange(Q)[:, None], idx4[np.arange(Q) % 128 // 16]] = pick8(a, idx3, 16)
    r = f1 - f2
    cc = b + r
    y = pick8(cc, idx5, 16)
    return y

@@ -1,0 +1,152 @@
+from contextlib import ExitStack
+
+import concourse.mybir as mybir
+
+D, K, T, U, SLOTS, Q = 512, 512, 1024, 1024, 512, 128
+FLOPS = 2 * D * K * Q + 2 * K * Q * T + 2 * K * Q * U
+
+F32 = mybir.dt.float32
+BF16 = mybir.dt.bfloat16
+I32 = mybir.dt.int32
+U32 = mybir.dt.uint32
+U16 = mybir.dt.uint16
+U8 = mybir.dt.uint8
+FP8X4 = mybir.dt.float8_e4m3fn_x4
+FP4X4 = mybir.dt.float4_e2m1fn_x4
+COPY = mybir.ActivationFunctionType.Copy
+ADD = mybir.AluOpType.add
+SUB = mybir.AluOpType.subtract
+
+P = 128
+PACK = 4
+LIST_COLS = SLOTS // 16
+A_TILE = 256
+B_TILE = 512
+
+
+def load_scale_rows(nc, plane, scales):
+    rows = scales[0].bitcast(I32)
+    dst = plane[:].bitcast(I32)
+    for r in range(4):
+        nc.sync.dma_start(out=dst[r:P:32, :], in_=rows[r:16:4, :])
+
+
+def tile_attend_withdrawn_madetwo_kernel(tc, states, wq_words, wq_scales, keys_words, keys_scales,
+                                          notes_words, notes_scales, offs, offs2, offs3, offs4, offs5, out):
+    nc = tc.nc
+    with ExitStack() as ctx:
+        sb = ctx.enter_context(tc.tile_pool(name="sb", bufs=1))
+        ps = ctx.enter_context(tc.psum_pool(name="ps", bufs=1))
+
+        wq_plane = sb.tile([P, K], U8, align_bytes=64)
+        keys_plane = sb.tile([P, T], U8, align_bytes=64)
+        notes_plane = sb.tile([P, U], U8, align_bytes=64)
+        f1 = sb.tile([P, U], F32, align_bytes=64)
+        f2 = sb.tile([P, U], F32, align_bytes=64)
+        nc.vector.memset(wq_plane[:].bitcast(U32), 0)
+        nc.vector.memset(keys_plane[:].bitcast(U32), 0)
+        nc.vector.memset(notes_plane[:].bitcast(U32), 0)
+        nc.vector.memset(f1[:], 0.0)
+        nc.vector.memset(f2[:], 0.0)
+
+        st_raw = sb.tile([P, PACK, Q], F32, align_bytes=64)
+        wq_raw = sb.tile([P, K], U32, align_bytes=64)
+        keys_sb = sb.tile([P, T], U32, align_bytes=64)
+        notes_sb = sb.tile([P, 2 * U], U8, align_bytes=64)
+        list1 = sb.tile([P, LIST_COLS], U16)
+        list2 = sb.tile([P, LIST_COLS], U16)
+        list3 = sb.tile([P, LIST_COLS], U16)
+        list4 = sb.tile([P, LIST_COLS], U16)
+        list5 = sb.tile([P, LIST_COLS], U16)
+
+        nc.sync.dma_start(out=st_raw[:], in_=states.rearrange("(p j) q -> p j q", j=PACK))
+        nc.sync.dma_start(out=wq_raw[:].bitcast(I32), in_=wq_words[0].rearrange("p n t -> p (n t)").bitcast(I32))
+        load_scale_rows(nc, wq_plane, wq_scales)
+        nc.sync.dma_start(out=keys_sb[:].bitcast(I32), in_=keys_words[0].rearrange("p n t -> p (n t)").bitcast(I32))
+        load_scale_rows(nc, keys_plane, keys_scales)
+        nc.sync.dma_start(list1[:], offs)
+        nc.sync.dma_start(list3[:], offs3)
+        nc.sync.dma_start(list2[:], offs2)
+        nc.sync.dma_start(list4[:], offs4)
+        nc.sync.dma_start(out=notes_sb[:].bitcast(I32), in_=notes_words[0].bitcast(I32))
+        load_scale_rows(nc, notes_plane, notes_scales)
+        nc.sync.dma_start(list5[:], offs5)
+
+        st_bf = sb.tile([P, Q, PACK], BF16, align_bytes=64)
+        st_view = st_raw[:].rearrange("p j q -> p q j")
+        half = Q // 2
+        nc.vector.tensor_copy(out=st_bf[:, 0:half, :], in_=st_view[:, 0:half, :])
+        nc.scalar.activation(out=st_bf[:, half:Q, :], in_=st_view[:, half:Q, :], func=COPY)
+
+        wq_plane_d = sb.tile([P, K], U8, align_bytes=64)
+        nc.vector.tensor_copy(out=wq_plane_d[:].rearrange("p (j m) -> p m j", j=PACK),
+                              in_=wq_plane[:].rearrange("p (m j) -> p m j", j=PACK))
+        st_codes = sb.tile([P, Q], U32, align_bytes=64)
+        st_plane = sb.tile([P, Q], U8, align_bytes=64)
+        nc.vector.quantize_mx(out=st_codes[:].bitcast(FP8X4), scales=st_plane[:],
+                              in_=st_bf[:].rearrange("p q j -> p (q j)"))
+
+        wq_d = sb.tile([P, K], U32, align_bytes=64)
+        src = wq_raw[:].rearrange("p (m j) -> p m j", j=PACK)
+        dst = wq_d[:].rearrange("p (j m) -> p m j", j=PACK)
+        nc.scalar.copy(out=dst[:, 0:half, :], in_=src[:, 0:half, :])
+        src_i = wq_raw[:].bitcast(I32).rearrange("p (m j) -> p m j", j=PACK)
+        dst_i = wq_d[:].bitcast(I32).rearrange("p (j m) -> p m j", j=PACK)
+        nc.vector.tensor_copy(out=dst_i[:, half:P, :], in_=src_i[:, half:P, :])
+
+        qv_ps = ps.tile([P, PACK, Q], F32)
+        for j in range(PACK):
+            cols = slice(j * P, (j + 1) * P)
+            nc.tensor.matmul_mx(out=qv_ps[:, j, :], lhsT=wq_d[:, cols].bitcast(FP8X4), lhsT_scale=wq_plane_d[:, cols],
+                                rhs=st_codes[:].bitcast(FP8X4), rhs_scale=st_plane[:], start=True, stop=True)
+        qv_bf = sb.tile([P, Q, PACK], BF16, align_bytes=64)
+        nc.scalar.activation(out=qv_bf[:], in_=qv_ps[:].rearrange("p j q -> p q j"), func=COPY)
+        qv_codes = sb.tile([P, Q], U32, align_bytes=64)
+        qv_plane = sb.tile([P, Q], U8, align_bytes=64)
+        nc.vector.quantize_mx(out=qv_codes[:].bitcast(FP8X4), scales=qv_plane[:],
+                              in_=qv_bf[:].rearrange("p q j -> p (q j)"))
+
+        a_sb = sb.tile([P, T], F32, align_bytes=64)
+        for n in range(T // A_TILE):
+            cols = slice(n * A_TILE, (n + 1) * A_TILE)
+            a_ps = ps.tile([P, A_TILE], F32, name="a_ps%d" % n)
+            nc.tensor.matmul_mx(out=a_ps[:], lhsT=qv_codes[:].bitcast(FP8X4), lhsT_scale=qv_plane[:],
+                                rhs=keys_sb[:, cols].bitcast(FP8X4), rhs_scale=keys_plane[:, cols],
+                                start=True, stop=True)
+            if n % 2 == 0:
+                nc.scalar.activation(out=a_sb[:, cols], in_=a_ps[:], func=COPY)
+            else:
+                nc.vector.tensor_copy(out=a_sb[:, cols], in_=a_ps[:])
+
+        hl = LIST_COLS // 2
+        hs = SLOTS // 2
+        pick1a = sb.tile([P, hs], F32, align_bytes=64)
+        pick1b = sb.tile([P, hs], F32, align_bytes=64)
+        pick3 = sb.tile([P, SLOTS], F32, align_bytes=64)
+        nc.vector.tensor_copy(pick1a[:], a_sb[:].indirect(list1[:, 0:hl]))
+        nc.scalar.activation(pick1b[:], a_sb[:].indirect(list1[:, hl:LIST_COLS]), COPY)
+        nc.scalar.activation(pick3[:], a_sb[:].indirect(list3[:]), COPY)
+        nc.vector.tensor_copy(f1[:].indirect(list2[:, 0:hl]), pick1a[:])
+        nc.vector.tensor_copy(f1[:].indirect(list2[:, hl:LIST_COLS]), pick1b[:])
+        nc.vector.tensor_copy(f2[:].indirect(list4[:]), pick3[:])
+
+        b_sb = sb.tile([P, U], F32, align_bytes=64)
+        for n in range(U // B_TILE):
+            cols = slice(n * B_TILE, (n + 1) * B_TILE)
+            b_ps = ps.tile([P, B_TILE], F32, name="b_ps%d" % n)
+            nc.tensor.matmul_mx(out=b_ps[:], lhsT=qv_codes[:].bitcast(FP8X4), lhsT_scale=qv_plane[:],
+                                rhs=notes_sb[:, 2 * n * B_TILE:2 * (n + 1) * B_TILE].bitcast(FP4X4),
+                                rhs_scale=notes_plane[:, cols], start=True, stop=True)
+            nc.scalar.activation(out=b_sb[:, cols], in_=b_ps[:], func=COPY)
+
+        bf1 = sb.tile([P, U], F32, align_bytes=64)
+        nc.gpsimd.tensor_tensor(out=bf1[:], in0=b_sb[:], in1=f1[:], op=ADD)
+        cc = sb.tile([P, U], F32, align_bytes=64)
+        nc.vector.tensor_tensor(out=cc[:], in0=bf1[:], in1=f2[:], op=SUB)
+
+        out_a = sb.tile([P, hs], F32, align_bytes=64)
+        out_b = sb.tile([P, hs], F32, align_bytes=64)
+        nc.vector.tensor_copy(out_a[:], cc[:].indirect(list5[:, 0:hl]))
+        nc.scalar.activation(out_b[:], cc[:].indirect(list5[:, hl:LIST_COLS]), COPY)
+        nc.sync.dma_start(out=out[:, 0:hs], in_=out_a[:])
+        nc.scalar.dma_start(out=out[:, hs:SLOTS], in_=out_b[:])

@@ -24,11 +24,11 @@ A_TILE = 256
 B_TILE = 512
 
 
-def load_scale_rows(nc, plane, scales):
+def load_scale_rows(queue, plane, scales):
     rows = scales[0].bitcast(I32)
     dst = plane[:].bitcast(I32)
     for r in range(4):
-        nc.sync.dma_start(out=dst[r:P:32, :], in_=rows[r:16:4, :])
+        queue.dma_start(out=dst[r:P:32, :], in_=rows[r:16:4, :])
 
 
 def tile_attend_withdrawn_madetwo_kernel(tc, states, wq_words, wq_scales, keys_words, keys_scales,
@@ -61,55 +61,57 @@ def tile_attend_withdrawn_madetwo_kernel(tc, states, wq_words, wq_scales, keys_w
 
         nc.sync.dma_start(out=st_raw[:], in_=states.rearrange("(p j) q -> p j q", j=PACK))
         nc.sync.dma_start(out=wq_raw[:].bitcast(I32), in_=wq_words[0].rearrange("p n t -> p (n t)").bitcast(I32))
-        load_scale_rows(nc, wq_plane, wq_scales)
-        nc.sync.dma_start(out=keys_sb[:].bitcast(I32), in_=keys_words[0].rearrange("p n t -> p (n t)").bitcast(I32))
-        load_scale_rows(nc, keys_plane, keys_scales)
+        load_scale_rows(nc.sync, wq_plane, wq_scales)
         nc.sync.dma_start(list1[:], offs)
+        nc.sync.dma_start(out=keys_sb[:].bitcast(I32), in_=keys_words[0].rearrange("p n t -> p (n t)").bitcast(I32))
+        load_scale_rows(nc.sync, keys_plane, keys_scales)
         nc.sync.dma_start(list3[:], offs3)
         nc.sync.dma_start(list2[:], offs2)
         nc.sync.dma_start(list4[:], offs4)
         nc.sync.dma_start(out=notes_sb[:].bitcast(I32), in_=notes_words[0].bitcast(I32))
-        load_scale_rows(nc, notes_plane, notes_scales)
+        load_scale_rows(nc.sync, notes_plane, notes_scales)
         nc.sync.dma_start(list5[:], offs5)
 
         st_bf = sb.tile([P, Q, PACK], BF16, align_bytes=64)
         st_view = st_raw[:].rearrange("p j q -> p q j")
         half = Q // 2
-        nc.vector.tensor_copy(out=st_bf[:, 0:half, :], in_=st_view[:, 0:half, :])
-        nc.scalar.activation(out=st_bf[:, half:Q, :], in_=st_view[:, half:Q, :], func=COPY)
+        nc.vector.tensor_copy(out=st_bf[:, 0:96, :], in_=st_view[:, 0:96, :])
+        nc.scalar.activation(out=st_bf[:, 96:Q, :], in_=st_view[:, 96:Q, :], func=COPY)
 
-        wq_plane_d = sb.tile([P, K], U8, align_bytes=64)
-        nc.vector.tensor_copy(out=wq_plane_d[:].rearrange("p (j m) -> p m j", j=PACK),
-                              in_=wq_plane[:].rearrange("p (m j) -> p m j", j=PACK))
         st_codes = sb.tile([P, Q], U32, align_bytes=64)
         st_plane = sb.tile([P, Q], U8, align_bytes=64)
         nc.vector.quantize_mx(out=st_codes[:].bitcast(FP8X4), scales=st_plane[:],
                               in_=st_bf[:].rearrange("p q j -> p (q j)"))
+        wq_pairs = []
+        plane_pairs = []
+        for h in range(2):
+            words_h = sb.tile([P, 2, P], U32, align_bytes=64, name="wq_d%d" % h)
+            plane_h = sb.tile([P, 2, P], U8, align_bytes=64, name="wq_plane_d%d" % h)
+            nc.scalar.copy(out=words_h[:].rearrange("p j m -> p m j"),
+                           in_=wq_raw[:].rearrange("p (m j) -> p m j", j=PACK)[:, :, 2 * h:2 * h + 2])
+            nc.vector.tensor_copy(out=plane_h[:].rearrange("p j m -> p m j"),
+                                  in_=wq_plane[:].rearrange("p (m j) -> p m j", j=PACK)[:, :, 2 * h:2 * h + 2])
+            wq_pairs.append(words_h)
+            plane_pairs.append(plane_h)
 
-        wq_d = sb.tile([P, K], U32, align_bytes=64)
-        src = wq_raw[:].rearrange("p (m j) -> p m j", j=PACK)
-        dst = wq_d[:].rearrange("p (j m) -> p m j", j=PACK)
-        nc.scalar.copy(out=dst[:, 0:half, :], in_=src[:, 0:half, :])
-        src_i = wq_raw[:].bitcast(I32).rearrange("p (m j) -> p m j", j=PACK)
-        dst_i = wq_d[:].bitcast(I32).rearrange("p (j m) -> p m j", j=PACK)
-        nc.vector.tensor_copy(out=dst_i[:, half:P, :], in_=src_i[:, half:P, :])
-
-        qv_ps = ps.tile([P, PACK, Q], F32)
+        qv_ps = [ps.tile([P, 2, Q], F32, name="qv_ps%d" % h, tag="shared%d" % h) for h in range(2)]
         for j in range(PACK):
-            cols = slice(j * P, (j + 1) * P)
-            nc.tensor.matmul_mx(out=qv_ps[:, j, :], lhsT=wq_d[:, cols].bitcast(FP8X4), lhsT_scale=wq_plane_d[:, cols],
+            nc.tensor.matmul_mx(out=qv_ps[j // 2][:, j % 2, :], lhsT=wq_pairs[j // 2][:, j % 2, :].bitcast(FP8X4),
+                                lhsT_scale=plane_pairs[j // 2][:, j % 2, :],
                                 rhs=st_codes[:].bitcast(FP8X4), rhs_scale=st_plane[:], start=True, stop=True)
         qv_bf = sb.tile([P, Q, PACK], BF16, align_bytes=64)
-        nc.scalar.activation(out=qv_bf[:], in_=qv_ps[:].rearrange("p j q -> p q j"), func=COPY)
+        nc.vector.tensor_copy(out=qv_bf[:, :, 0:2], in_=qv_ps[0][:].rearrange("p j q -> p q j"))
+        nc.scalar.activation(out=qv_bf[:, :, 2:4], in_=qv_ps[1][:].rearrange("p j q -> p q j"), func=COPY)
         qv_codes = sb.tile([P, Q], U32, align_bytes=64)
         qv_plane = sb.tile([P, Q], U8, align_bytes=64)
         nc.vector.quantize_mx(out=qv_codes[:].bitcast(FP8X4), scales=qv_plane[:],
                               in_=qv_bf[:].rearrange("p q j -> p (q j)"))
 
         a_sb = sb.tile([P, T], F32, align_bytes=64)
-        for n in range(T // A_TILE):
-            cols = slice(n * A_TILE, (n + 1) * A_TILE)
-            a_ps = ps.tile([P, A_TILE], F32, name="a_ps%d" % n)
+        edges = [0, 256, 512, 768, 896, 1024]
+        for n in range(len(edges) - 1):
+            cols = slice(edges[n], edges[n + 1])
+            a_ps = ps.tile([P, edges[n + 1] - edges[n]], F32, name="a_ps%d" % n)
             nc.tensor.matmul_mx(out=a_ps[:], lhsT=qv_codes[:].bitcast(FP8X4), lhsT_scale=qv_plane[:],
                                 rhs=keys_sb[:, cols].bitcast(FP8X4), rhs_scale=keys_plane[:, cols],
                                 start=True, stop=True)
@@ -120,20 +122,18 @@ def tile_attend_withdrawn_madetwo_kernel(tc, states, wq_words, wq_scales, keys_w
 
         hl = LIST_COLS // 2
         hs = SLOTS // 2
-        pick1a = sb.tile([P, hs], F32, align_bytes=64)
-        pick1b = sb.tile([P, hs], F32, align_bytes=64)
+        pick1 = sb.tile([P, SLOTS], F32, align_bytes=64)
         pick3 = sb.tile([P, SLOTS], F32, align_bytes=64)
-        nc.vector.tensor_copy(pick1a[:], a_sb[:].indirect(list1[:, 0:hl]))
-        nc.scalar.activation(pick1b[:], a_sb[:].indirect(list1[:, hl:LIST_COLS]), COPY)
+        nc.vector.tensor_copy(pick1[:, 0:hs], a_sb[:].indirect(list1[:, 0:hl]))
+        nc.scalar.activation(pick1[:, hs:SLOTS], a_sb[:].indirect(list1[:, hl:LIST_COLS]), COPY)
         nc.scalar.activation(pick3[:], a_sb[:].indirect(list3[:]), COPY)
-        nc.vector.tensor_copy(f1[:].indirect(list2[:, 0:hl]), pick1a[:])
-        nc.vector.tensor_copy(f1[:].indirect(list2[:, hl:LIST_COLS]), pick1b[:])
+        nc.vector.tensor_copy(f1[:].indirect(list2[:]), pick1[:])
         nc.vector.tensor_copy(f2[:].indirect(list4[:]), pick3[:])
 
         b_sb = sb.tile([P, U], F32, align_bytes=64)
         for n in range(U // B_TILE):
             cols = slice(n * B_TILE, (n + 1) * B_TILE)
-            b_ps = ps.tile([P, B_TILE], F32, name="b_ps%d" % n)
+            b_ps = ps.tile([P, B_TILE], F32, name="b_ps%d" % n, tag="shared%d" % n)
             nc.tensor.matmul_mx(out=b_ps[:], lhsT=qv_codes[:].bitcast(FP8X4), lhsT_scale=qv_plane[:],
                                 rhs=notes_sb[:, 2 * n * B_TILE:2 * (n + 1) * B_TILE].bitcast(FP4X4),
                                 rhs_scale=notes_plane[:, cols], start=True, stop=True)

@@ -1,6 +1,7 @@
 from contextlib import ExitStack
 
 import concourse.mybir as mybir
+from concourse.masks import make_identity
 
 D, K, T, U, SLOTS, Q = 512, 512, 1024, 1024, 512, 128
 FLOPS = 2 * D * K * Q + 2 * K * Q * T + 2 * K * Q * U
@@ -42,12 +43,15 @@ def tile_attend_withdrawn_madetwo_kernel(tc, states, wq_words, wq_scales, keys_w
         keys_plane = sb.tile([P, T], U8, align_bytes=64)
         notes_plane = sb.tile([P, U], U8, align_bytes=64)
         f1 = sb.tile([P, U], F32, align_bytes=64)
-        f2 = sb.tile([P, U], F32, align_bytes=64)
         nc.vector.memset(wq_plane[:].bitcast(U32), 0)
+        ident = sb.tile([P, P], F32, align_bytes=64)
+        nc.vector.memset(ident[:], 0.0)
+        make_identity(nc, ident[:], nomemset=True)
         nc.vector.memset(keys_plane[:].bitcast(U32), 0)
         nc.vector.memset(notes_plane[:].bitcast(U32), 0)
+        ones = sb.tile([P, 128], F32, align_bytes=64)
+        nc.vector.memset(ones[:], 1.0)
         nc.vector.memset(f1[:], 0.0)
-        nc.vector.memset(f2[:], 0.0)
 
         st_raw = sb.tile([P, PACK, Q], F32, align_bytes=64)
         wq_raw = sb.tile([P, K], U32, align_bytes=64)
@@ -99,7 +103,7 @@ def tile_attend_withdrawn_madetwo_kernel(tc, states, wq_words, wq_scales, keys_w
             nc.tensor.matmul_mx(out=qv_ps[j // 2][:, j % 2, :], lhsT=wq_pairs[j // 2][:, j % 2, :].bitcast(FP8X4),
                                 lhsT_scale=plane_pairs[j // 2][:, j % 2, :],
                                 rhs=st_codes[:].bitcast(FP8X4), rhs_scale=st_plane[:], start=True, stop=True)
-        qv_bf = sb.tile([P, Q, PACK], BF16, align_bytes=64)
+        qv_bf = sb.tile([P, Q, PACK], BF16, align_bytes=64, tag="qv_then_f2")
         nc.vector.tensor_copy(out=qv_bf[:, :, 0:2], in_=qv_ps[0][:].rearrange("p j q -> p q j"))
         nc.scalar.activation(out=qv_bf[:, :, 2:4], in_=qv_ps[1][:].rearrange("p j q -> p q j"), func=COPY)
         qv_codes = sb.tile([P, Q], U32, align_bytes=64)
@@ -107,11 +111,14 @@ def tile_attend_withdrawn_madetwo_kernel(tc, states, wq_words, wq_scales, keys_w
         nc.vector.quantize_mx(out=qv_codes[:].bitcast(FP8X4), scales=qv_plane[:],
                               in_=qv_bf[:].rearrange("p q j -> p (q j)"))
 
+        f2 = sb.tile([P, U], F32, align_bytes=64, tag="qv_then_f2")
+        nc.vector.memset(f2[:], 0.0)
+
         a_sb = sb.tile([P, T], F32, align_bytes=64)
         edges = [0, 256, 512, 768, 896, 1024]
         for n in range(len(edges) - 1):
             cols = slice(edges[n], edges[n + 1])
-            a_ps = ps.tile([P, edges[n + 1] - edges[n]], F32, name="a_ps%d" % n)
+            a_ps = ps.tile([P, edges[n + 1] - edges[n]], F32, name="a_ps%d" % n, tag="score%d" % n)
             nc.tensor.matmul_mx(out=a_ps[:], lhsT=qv_codes[:].bitcast(FP8X4), lhsT_scale=qv_plane[:],
                                 rhs=keys_sb[:, cols].bitcast(FP8X4), rhs_scale=keys_plane[:, cols],
                                 start=True, stop=True)
@@ -122,13 +129,17 @@ def tile_attend_withdrawn_madetwo_kernel(tc, states, wq_words, wq_scales, keys_w
 
         hl = LIST_COLS // 2
         hs = SLOTS // 2
-        pick1 = sb.tile([P, SLOTS], F32, align_bytes=64)
+        pick1a = sb.tile([P, 128], F32, align_bytes=64)
+        pick1b = sb.tile([P, 384], F32, align_bytes=64)
         pick3 = sb.tile([P, SLOTS], F32, align_bytes=64)
-        nc.vector.tensor_copy(pick1[:, 0:hs], a_sb[:].indirect(list1[:, 0:hl]))
-        nc.scalar.activation(pick1[:, hs:SLOTS], a_sb[:].indirect(list1[:, hl:LIST_COLS]), COPY)
-        nc.scalar.activation(pick3[:], a_sb[:].indirect(list3[:]), COPY)
-        nc.vector.tensor_copy(f1[:].indirect(list2[:]), pick1[:])
-        nc.vector.tensor_copy(f2[:].indirect(list4[:]), pick3[:])
+        nc.vector.tensor_tensor(pick1a[:], a_sb[:].indirect(list1[:, 0:8]), ones[:], mybir.AluOpType.mult)
+        nc.scalar.activation(pick3[:, 0:hs], a_sb[:].indirect(list3[:, 0:hl]), COPY)
+        nc.scalar.activation(pick1b[:], a_sb[:].indirect(list1[:, 8:LIST_COLS]), COPY)
+        nc.scalar.activation(pick3[:, hs:SLOTS], a_sb[:].indirect(list3[:, hl:LIST_COLS]), COPY)
+        nc.vector.tensor_copy(f1[:].indirect(list2[:, 0:8]), pick1a[:])
+        nc.vector.tensor_copy(f2[:].indirect(list4[:, 0:8]), pick3[:, 0:128])
+        nc.vector.tensor_copy(f1[:].indirect(list2[:, 8:LIST_COLS]), pick1b[:])
+        nc.vector.tensor_copy(f2[:].indirect(list4[:, 8:LIST_COLS]), pick3[:, 128:SLOTS])
 
         b_sb = sb.tile([P, U], F32, align_bytes=64)
         for n in range(U // B_TILE):
@@ -139,10 +150,32 @@ def tile_attend_withdrawn_madetwo_kernel(tc, states, wq_words, wq_scales, keys_w
                                 rhs_scale=notes_plane[:, cols], start=True, stop=True)
             nc.scalar.activation(out=b_sb[:, cols], in_=b_ps[:], func=COPY)
 
-        bf1 = sb.tile([P, U], F32, align_bytes=64)
-        nc.gpsimd.tensor_tensor(out=bf1[:], in0=b_sb[:], in1=f1[:], op=ADD)
         cc = sb.tile([P, U], F32, align_bytes=64)
-        nc.vector.tensor_tensor(out=cc[:], in0=bf1[:], in1=f2[:], op=SUB)
+        spans = [(0, 256), (256, 512), (512, 768)]
+        turned = []
+        for n, (lo, hi) in enumerate(spans):
+            blocks = range(lo, hi, P)
+            t_ps = ps.tile([P, hi - lo], F32, name="t_ps%d" % n, tag="score%d" % n)
+            for c in blocks:
+                nc.tensor.matmul(t_ps[:, c - lo:c - lo + P], lhsT=b_sb[:, c:c + P], rhs=ident[:], is_transpose=True,
+                                 start=(c == lo), stop=False)
+            turned.append(t_ps)
+        t_sb = sb.tile([P, 768], F32, align_bytes=64)
+        for n, (lo, hi) in enumerate(spans):
+            blocks = range(lo, hi, P)
+            for c in blocks:
+                nc.tensor.matmul(turned[n][:, c - lo:c - lo + P], lhsT=f1[:, c:c + P], rhs=ident[:], is_transpose=True,
+                                 start=False, stop=(c == hi - P))
+            nc.scalar.activation(out=t_sb[:, lo:hi], in_=turned[n][:], func=COPY)
+        rest = slice(768, U)
+        bf1 = sb.tile([P, U - 768], F32, align_bytes=64)
+        nc.gpsimd.tensor_tensor(out=bf1[:], in0=b_sb[:, rest], in1=f1[:, rest], op=ADD)
+        for n, (lo, hi) in enumerate([(0, 512), (512, 768)]):
+            g_ps = ps.tile([P, hi - lo], F32, name="g_ps%d" % n, tag="score%d" % (3 + n))
+            for c in range(lo, hi, P):
+                nc.tensor.transpose(g_ps[:, c - lo:c - lo + P], t_sb[:, c:c + P], ident[:])
+            nc.vector.tensor_tensor(out=cc[:, lo:hi], in0=g_ps[:], in1=f2[:, lo:hi], op=SUB)
+        nc.gpsimd.tensor_tensor(out=cc[:, rest], in0=bf1[:], in1=f2[:, rest], op=mybir.AluOpType.subtract)
 
         out_a = sb.tile([P, hs], F32, align_bytes=64)
         out_b = sb.tile([P, hs], F32, align_bytes=64)

@@ -90,18 +90,18 @@ def tile_attend_withdrawn_madetwo_kernel(tc, states, wq_words, wq_scales, keys_w
         plane_pairs = []
         for h in range(2):
             words_h = sb.tile([P, 2, P], U32, align_bytes=64, name="wq_d%d" % h)
-            plane_h = sb.tile([P, 2, P], U8, align_bytes=64, name="wq_plane_d%d" % h)
             nc.scalar.copy(out=words_h[:].rearrange("p j m -> p m j"),
                            in_=wq_raw[:].rearrange("p (m j) -> p m j", j=PACK)[:, :, 2 * h:2 * h + 2])
-            nc.vector.tensor_copy(out=plane_h[:].rearrange("p j m -> p m j"),
-                                  in_=wq_plane[:].rearrange("p (m j) -> p m j", j=PACK)[:, :, 2 * h:2 * h + 2])
             wq_pairs.append(words_h)
-            plane_pairs.append(plane_h)
+        for j in range(PACK):
+            plane_j = sb.tile([P, P], U8, align_bytes=64, name="wq_plane_d%d" % j)
+            nc.vector.tensor_copy(out=plane_j[:], in_=wq_plane[:, j:K:PACK])
+            plane_pairs.append(plane_j)
 
         qv_ps = [ps.tile([P, 2, Q], F32, name="qv_ps%d" % h, tag="shared%d" % h) for h in range(2)]
         for j in range(PACK):
             nc.tensor.matmul_mx(out=qv_ps[j // 2][:, j % 2, :], lhsT=wq_pairs[j // 2][:, j % 2, :].bitcast(FP8X4),
-                                lhsT_scale=plane_pairs[j // 2][:, j % 2, :],
+                                lhsT_scale=plane_pairs[j][:],
                                 rhs=st_codes[:].bitcast(FP8X4), rhs_scale=st_plane[:], start=True, stop=True)
         qv_bf = sb.tile([P, Q, PACK], BF16, align_bytes=64, tag="qv_then_f2")
         nc.vector.tensor_copy(out=qv_bf[:, :, 0:2], in_=qv_ps[0][:].rearrange("p j q -> p q j"))
@@ -151,7 +151,7 @@ def tile_attend_withdrawn_madetwo_kernel(tc, states, wq_words, wq_scales, keys_w
             nc.scalar.activation(out=b_sb[:, cols], in_=b_ps[:], func=COPY)
 
         cc = sb.tile([P, U], F32, align_bytes=64)
-        spans = [(0, 256), (256, 512), (512, 768)]
+        spans = [(0, 256), (256, 512), (512, 640)]
         turned = []
         for n, (lo, hi) in enumerate(spans):
             blocks = range(lo, hi, P)
@@ -160,18 +160,18 @@ def tile_attend_withdrawn_madetwo_kernel(tc, states, wq_words, wq_scales, keys_w
                 nc.tensor.matmul(t_ps[:, c - lo:c - lo + P], lhsT=b_sb[:, c:c + P], rhs=ident[:], is_transpose=True,
                                  start=(c == lo), stop=False)
             turned.append(t_ps)
-        t_sb = sb.tile([P, 768], F32, align_bytes=64)
+        t_sb = sb.tile([P, 640], F32, align_bytes=64)
         for n, (lo, hi) in enumerate(spans):
             blocks = range(lo, hi, P)
             for c in blocks:
                 nc.tensor.matmul(turned[n][:, c - lo:c - lo + P], lhsT=f1[:, c:c + P], rhs=ident[:], is_transpose=True,
                                  start=False, stop=(c == hi - P))
             nc.scalar.activation(out=t_sb[:, lo:hi], in_=turned[n][:], func=COPY)
-        rest = slice(768, U)
-        bf1 = sb.tile([P, U - 768], F32, align_bytes=64)
+        rest = slice(640, U)
+        bf1 = sb.tile([P, U - 640], F32, align_bytes=64)
         nc.gpsimd.tensor_tensor(out=bf1[:], in0=b_sb[:, rest], in1=f1[:, rest], op=ADD)
-        for n, (lo, hi) in enumerate([(0, 512), (512, 768)]):
-            g_ps = ps.tile([P, hi - lo], F32, name="g_ps%d" % n, tag="score%d" % (3 + n))
+        for n, (lo, hi) in enumerate(spans):
+            g_ps = ps.tile([P, hi - lo], F32, name="g_ps%d" % n, tag=["score3", "score4", "shared0"][n])
             for c in range(lo, hi, P):
                 nc.tensor.transpose(g_ps[:, c - lo:c - lo + P], t_sb[:, c:c + P], ident[:])
             nc.vector.tensor_tensor(out=cc[:, lo:hi], in0=g_ps[:], in1=f2[:, lo:hi], op=SUB)

from contextlib import ExitStack

import concourse.mybir as mybir
from concourse.masks import make_identity

D, K, T, U, SLOTS, Q = 512, 512, 1024, 1024, 512, 128
FLOPS = 2 * D * K * Q + 2 * K * Q * T + 2 * K * Q * U

F32 = mybir.dt.float32
BF16 = mybir.dt.bfloat16
I32 = mybir.dt.int32
U32 = mybir.dt.uint32
U16 = mybir.dt.uint16
U8 = mybir.dt.uint8
FP8X4 = mybir.dt.float8_e4m3fn_x4
FP4X4 = mybir.dt.float4_e2m1fn_x4
COPY = mybir.ActivationFunctionType.Copy
ADD = mybir.AluOpType.add
SUB = mybir.AluOpType.subtract

P = 128
PACK = 4
LIST_COLS = SLOTS // 16
A_TILE = 256
B_TILE = 512


def load_scale_rows(queue, plane, scales):
    rows = scales[0].bitcast(I32)
    dst = plane[:].bitcast(I32)
    for r in range(4):
        queue.dma_start(out=dst[r:P:32, :], in_=rows[r:16:4, :])


def tile_attend_withdrawn_madetwo_kernel(tc, states, wq_words, wq_scales, keys_words, keys_scales,
                                          notes_words, notes_scales, offs, offs2, offs3, offs4, offs5, out):
    nc = tc.nc
    with ExitStack() as ctx:
        sb = ctx.enter_context(tc.tile_pool(name="sb", bufs=1))
        ps = ctx.enter_context(tc.psum_pool(name="ps", bufs=1))

        wq_plane = sb.tile([P, K], U8, align_bytes=64)
        keys_plane = sb.tile([P, T], U8, align_bytes=64)
        notes_plane = sb.tile([P, U], U8, align_bytes=64)
        f1 = sb.tile([P, U], F32, align_bytes=64)
        nc.vector.memset(wq_plane[:].bitcast(U32), 0)
        ident = sb.tile([P, P], F32, align_bytes=64)
        nc.vector.memset(ident[:], 0.0)
        make_identity(nc, ident[:], nomemset=True)
        nc.vector.memset(keys_plane[:].bitcast(U32), 0)
        nc.vector.memset(notes_plane[:].bitcast(U32), 0)
        ones = sb.tile([P, 128], F32, align_bytes=64)
        nc.vector.memset(ones[:], 1.0)
        nc.vector.memset(f1[:], 0.0)

        st_raw = sb.tile([P, PACK, Q], F32, align_bytes=64)
        wq_raw = sb.tile([P, K], U32, align_bytes=64)
        keys_sb = sb.tile([P, T], U32, align_bytes=64)
        notes_sb = sb.tile([P, 2 * U], U8, align_bytes=64)
        list1 = sb.tile([P, LIST_COLS], U16)
        list2 = sb.tile([P, LIST_COLS], U16)
        list3 = sb.tile([P, LIST_COLS], U16)
        list4 = sb.tile([P, LIST_COLS], U16)
        list5 = sb.tile([P, LIST_COLS], U16)

        nc.sync.dma_start(out=st_raw[:], in_=states.rearrange("(p j) q -> p j q", j=PACK))
        nc.sync.dma_start(out=wq_raw[:].bitcast(I32), in_=wq_words[0].rearrange("p n t -> p (n t)").bitcast(I32))
        load_scale_rows(nc.sync, wq_plane, wq_scales)
        nc.sync.dma_start(list1[:], offs)
        nc.sync.dma_start(out=keys_sb[:].bitcast(I32), in_=keys_words[0].rearrange("p n t -> p (n t)").bitcast(I32))
        load_scale_rows(nc.sync, keys_plane, keys_scales)
        nc.sync.dma_start(list3[:], offs3)
        nc.sync.dma_start(list2[:], offs2)
        nc.sync.dma_start(list4[:], offs4)
        nc.sync.dma_start(out=notes_sb[:].bitcast(I32), in_=notes_words[0].bitcast(I32))
        load_scale_rows(nc.sync, notes_plane, notes_scales)
        nc.sync.dma_start(list5[:], offs5)

        st_bf = sb.tile([P, Q, PACK], BF16, align_bytes=64)
        st_view = st_raw[:].rearrange("p j q -> p q j")
        half = Q // 2
        nc.vector.tensor_copy(out=st_bf[:, 0:96, :], in_=st_view[:, 0:96, :])
        nc.scalar.activation(out=st_bf[:, 96:Q, :], in_=st_view[:, 96:Q, :], func=COPY)

        st_codes = sb.tile([P, Q], U32, align_bytes=64)
        st_plane = sb.tile([P, Q], U8, align_bytes=64)
        nc.vector.quantize_mx(out=st_codes[:].bitcast(FP8X4), scales=st_plane[:],
                              in_=st_bf[:].rearrange("p q j -> p (q j)"))
        wq_pairs = []
        plane_pairs = []
        for h in range(2):
            words_h = sb.tile([P, 2, P], U32, align_bytes=64, name="wq_d%d" % h)
            nc.scalar.copy(out=words_h[:].rearrange("p j m -> p m j"),
                           in_=wq_raw[:].rearrange("p (m j) -> p m j", j=PACK)[:, :, 2 * h:2 * h + 2])
            wq_pairs.append(words_h)
        for j in range(PACK):
            plane_j = sb.tile([P, P], U8, align_bytes=64, name="wq_plane_d%d" % j)
            nc.vector.tensor_copy(out=plane_j[:], in_=wq_plane[:, j:K:PACK])
            plane_pairs.append(plane_j)

        qv_ps = [ps.tile([P, 2, Q], F32, name="qv_ps%d" % h, tag="shared%d" % h) for h in range(2)]
        for j in range(PACK):
            nc.tensor.matmul_mx(out=qv_ps[j // 2][:, j % 2, :], lhsT=wq_pairs[j // 2][:, j % 2, :].bitcast(FP8X4),
                                lhsT_scale=plane_pairs[j][:],
                                rhs=st_codes[:].bitcast(FP8X4), rhs_scale=st_plane[:], start=True, stop=True)
        qv_bf = sb.tile([P, Q, PACK], BF16, align_bytes=64, tag="qv_then_f2")
        nc.vector.tensor_copy(out=qv_bf[:, :, 0:2], in_=qv_ps[0][:].rearrange("p j q -> p q j"))
        nc.scalar.activation(out=qv_bf[:, :, 2:4], in_=qv_ps[1][:].rearrange("p j q -> p q j"), func=COPY)
        qv_codes = sb.tile([P, Q], U32, align_bytes=64)
        qv_plane = sb.tile([P, Q], U8, align_bytes=64)
        nc.vector.quantize_mx(out=qv_codes[:].bitcast(FP8X4), scales=qv_plane[:],
                              in_=qv_bf[:].rearrange("p q j -> p (q j)"))

        f2 = sb.tile([P, U], F32, align_bytes=64, tag="qv_then_f2")
        nc.vector.memset(f2[:], 0.0)

        a_sb = sb.tile([P, T], F32, align_bytes=64)
        edges = [0, 256, 512, 768, 896, 1024]
        for n in range(len(edges) - 1):
            cols = slice(edges[n], edges[n + 1])
            a_ps = ps.tile([P, edges[n + 1] - edges[n]], F32, name="a_ps%d" % n, tag="score%d" % n)
            nc.tensor.matmul_mx(out=a_ps[:], lhsT=qv_codes[:].bitcast(FP8X4), lhsT_scale=qv_plane[:],
                                rhs=keys_sb[:, cols].bitcast(FP8X4), rhs_scale=keys_plane[:, cols],
                                start=True, stop=True)
            if n % 2 == 0:
                nc.scalar.activation(out=a_sb[:, cols], in_=a_ps[:], func=COPY)
            else:
                nc.vector.tensor_copy(out=a_sb[:, cols], in_=a_ps[:])

        hl = LIST_COLS // 2
        hs = SLOTS // 2
        pick1a = sb.tile([P, 128], F32, align_bytes=64)
        pick1b = sb.tile([P, 384], F32, align_bytes=64)
        pick3 = sb.tile([P, SLOTS], F32, align_bytes=64)
        nc.vector.tensor_tensor(pick1a[:], a_sb[:].indirect(list1[:, 0:8]), ones[:], mybir.AluOpType.mult)
        nc.scalar.activation(pick3[:, 0:hs], a_sb[:].indirect(list3[:, 0:hl]), COPY)
        nc.scalar.activation(pick1b[:], a_sb[:].indirect(list1[:, 8:LIST_COLS]), COPY)
        nc.scalar.activation(pick3[:, hs:SLOTS], a_sb[:].indirect(list3[:, hl:LIST_COLS]), COPY)
        nc.vector.tensor_copy(f1[:].indirect(list2[:, 0:8]), pick1a[:])
        nc.vector.tensor_copy(f2[:].indirect(list4[:, 0:8]), pick3[:, 0:128])
        nc.vector.tensor_copy(f1[:].indirect(list2[:, 8:LIST_COLS]), pick1b[:])
        nc.vector.tensor_copy(f2[:].indirect(list4[:, 8:LIST_COLS]), pick3[:, 128:SLOTS])

        b_sb = sb.tile([P, U], F32, align_bytes=64)
        for n in range(U // B_TILE):
            cols = slice(n * B_TILE, (n + 1) * B_TILE)
            b_ps = ps.tile([P, B_TILE], F32, name="b_ps%d" % n, tag="shared%d" % n)
            nc.tensor.matmul_mx(out=b_ps[:], lhsT=qv_codes[:].bitcast(FP8X4), lhsT_scale=qv_plane[:],
                                rhs=notes_sb[:, 2 * n * B_TILE:2 * (n + 1) * B_TILE].bitcast(FP4X4),
                                rhs_scale=notes_plane[:, cols], start=True, stop=True)
            nc.scalar.activation(out=b_sb[:, cols], in_=b_ps[:], func=COPY)

        cc = sb.tile([P, U], F32, align_bytes=64)
        spans = [(0, 256), (256, 512), (512, 640)]
        turned = []
        for n, (lo, hi) in enumerate(spans):
            blocks = range(lo, hi, P)
            t_ps = ps.tile([P, hi - lo], F32, name="t_ps%d" % n, tag="score%d" % n)
            for c in blocks:
                nc.tensor.matmul(t_ps[:, c - lo:c - lo + P], lhsT=b_sb[:, c:c + P], rhs=ident[:], is_transpose=True,
                                 start=(c == lo), stop=False)
            turned.append(t_ps)
        t_sb = sb.tile([P, 640], F32, align_bytes=64)
        for n, (lo, hi) in enumerate(spans):
            blocks = range(lo, hi, P)
            for c in blocks:
                nc.tensor.matmul(turned[n][:, c - lo:c - lo + P], lhsT=f1[:, c:c + P], rhs=ident[:], is_transpose=True,
                                 start=False, stop=(c == hi - P))
            nc.scalar.activation(out=t_sb[:, lo:hi], in_=turned[n][:], func=COPY)
        rest = slice(640, U)
        bf1 = sb.tile([P, U - 640], F32, align_bytes=64)
        nc.gpsimd.tensor_tensor(out=bf1[:], in0=b_sb[:, rest], in1=f1[:, rest], op=ADD)
        for n, (lo, hi) in enumerate(spans):
            g_ps = ps.tile([P, hi - lo], F32, name="g_ps%d" % n, tag=["score3", "score4", "shared0"][n])
            for c in range(lo, hi, P):
                nc.tensor.transpose(g_ps[:, c - lo:c - lo + P], t_sb[:, c:c + P], ident[:])
            nc.vector.tensor_tensor(out=cc[:, lo:hi], in0=g_ps[:], in1=f2[:, lo:hi], op=SUB)
        nc.gpsimd.tensor_tensor(out=cc[:, rest], in0=bf1[:], in1=f2[:, rest], op=mybir.AluOpType.subtract)

        out_a = sb.tile([P, hs], F32, align_bytes=64)
        out_b = sb.tile([P, hs], F32, align_bytes=64)
        nc.vector.tensor_copy(out_a[:], cc[:].indirect(list5[:, 0:hl]))
        nc.scalar.activation(out_b[:], cc[:].indirect(list5[:, hl:LIST_COLS]), COPY)
        nc.sync.dma_start(out=out[:, 0:hs], in_=out_a[:])
        nc.scalar.dma_start(out=out[:, hs:SLOTS], in_=out_b[:])
